import numpy as np
import ml_dtypes


def mxq(x, axis, fmt="e4m3"):
    dtype, down = {"e4m3": (ml_dtypes.float8_e4m3fn, 7), "e5m2": (ml_dtypes.float8_e5m2, 14)}[fmt]
    v = np.moveaxis(np.asarray(x, np.float32).astype(ml_dtypes.bfloat16).astype(np.float64), axis, -1)
    blocks = v.reshape(v.shape[:-1] + (-1, 32))
    amax = np.abs(blocks).max(-1, keepdims=True)
    byte = np.maximum(np.where(amax > 0, np.frexp(amax)[1] - 1 + 127, 0) - down, 1)
    scale = np.exp2(byte - 127.0)
    codes = (blocks / scale).astype(np.float32).astype(dtype).astype(np.float64)
    return np.moveaxis((codes * scale).reshape(v.shape), -1, axis)


WIDE = False


def mx_kscale(k):
    if not WIDE:
        return np.ones(k)
    levels = np.array([10, -10, 5, -5, 0])
    if k % 512:
        return np.exp2(np.random.permutation(np.resize(levels, k // 32))).repeat(32)
    a = np.empty((k // 512, 16))
    for p in range(k // 512):
        a[p, :8] = np.random.permutation(np.resize(levels, 8))
        for g in range(8):
            far = levels[np.abs(levels - a[p, g]) >= 10]
            a[p, g + 8] = far[np.random.randint(len(far))]
    return np.exp2(a.ravel()).repeat(32)


def f64(x):
    return np.asarray(x).astype(np.float64)


def striped(idx):
    return np.tile(idx.reshape(-1, 16).T, (8, 1)).astype(np.uint16)


def unstriped(offs):
    return offs[:16].T.reshape(-1).astype(np.int64)


def pack_weight(w):
    k, n = w.shape
    w = f64(np.asarray(w, np.float32).astype(ml_dtypes.bfloat16)).reshape(k // 32, 32, n)
    amax = np.abs(w).max(1)
    byte = np.clip(np.where(amax > 0, np.frexp(amax)[1] - 1 + 127 - 7, 1), 1, 254)
    scaled = (w * np.exp2(127.0 - byte)[:, None, :]).reshape(k, n).astype(np.float32)
    words = np.ascontiguousarray(scaled.reshape(k // 512, 128, 4, n).transpose(0, 1, 3, 2)).astype(ml_dtypes.float8_e4m3fn).view(np.uint8)
    return words, np.ascontiguousarray(byte.astype(np.uint8).reshape(k // 512, 16, n))


def unpack_weight(words, scales):
    g, p, n, _ = words.shape
    vals = np.ascontiguousarray(words).view(ml_dtypes.float8_e4m3fn).astype(np.float64) * np.repeat(np.exp2(scales.astype(np.float64) - 127.0), 8, axis=1)[..., None]
    return vals.transpose(0, 1, 3, 2).reshape(g * 512, n)


def sigmoid(v):
    return 1.0 / (1.0 + np.exp(-np.maximum(v, -700.0)))


K, T, S, V = 512, 2048, 512, 512
P = 2 ** 7


def setup_inputs():
    n = np.random.standard_normal
    s = mx_kscale(K)[:, None]
    packed_xT = pack_weight(n((K, T)) * s)
    packed_eT = pack_weight(n((K, T)) * s)
    return {
        "x_words": packed_xT[0],
        "x_scales": packed_xT[1],
        "hT": (n((K, V)) / np.sqrt(K) / s).astype(np.float32),
        "e_words": packed_eT[0],
        "e_scales": packed_eT[1],
        "lib": (np.random.uniform(200.0, 800.0, (V, 1))).astype(np.float32),
        "theta": (np.tile(np.random.uniform(0.5, 3.0, T), (P, 1))).astype(np.float32),
        "cnt": (np.floor(np.random.uniform(0.0, 1.0, (V, S)) ** 3 * 6)).astype(np.float32),
        "zero": ((np.random.uniform(size=(V, S)) < 0.4) * 1.0).astype(np.float32),
        "offs": striped(np.random.permutation(T)[:S]),
    }


def reference(x_words, x_scales, hT, e_words, e_scales, lib, theta, cnt, zero, offs):
    hTq = mxq(f64(hT), 0, "e4m3")
    xq = unpack_weight(x_words, x_scales)[:, unstriped(offs)]
    y = hTq.T @ xq
    ex = np.exp(y - y.max(axis=1, keepdims=True))
    mu = f64(lib) * (ex / ex.sum(axis=1, keepdims=True))
    lt = np.log(f64(theta)[:1][:, unstriped(offs)]) - (np.log(f64(theta)[:1][:, unstriped(offs)] + mu))
    nb1 = lt * (f64(theta)[:1][:, unstriped(offs)]) + f64(cnt) * (np.log(mu + 0.001) - (np.log(f64(theta)[:1][:, unstriped(offs)] + mu)))
    e_offs = unpack_weight(e_words, e_scales)[:, unstriped(offs)]
    pi = hTq.T @ e_offs
    sg = sigmoid(pi)
    l1 = nb1 + np.log(-1.0 * sg + 1.0001)
    l0 = np.log(sg + (np.exp(lt * (f64(theta)[:1][:, unstriped(offs)]))) * (-1.0 * sg + 1.0))
    return l1 + f64(zero) * (l0 - l1)

@@ -1,0 +1,244 @@
+from contextlib import ExitStack
+
+import concourse.mybir as mybir
+from concourse.masks import make_identity
+
+F32 = mybir.dt.float32
+BF16 = mybir.dt.bfloat16
+I32 = mybir.dt.int32
+U32 = mybir.dt.uint32
+U16 = mybir.dt.uint16
+U8 = mybir.dt.uint8
+FP8X4 = mybir.dt.float8_e4m3fn_x4
+ACT = mybir.ActivationFunctionType
+ALU = mybir.AluOpType
+AX = mybir.AxisListType
+
+P = 128
+K = 512
+T = 2048
+S = 512
+V = 512
+PACK = 4
+NB = 4
+HALF = V // 2
+
+FLOPS = 2 * 2 * K * V * S
+
+
+def tile_picked_yzinb_ll_p_kernel(
+    tc, x_words, x_scales, hT, e_words, e_scales, lib, theta, cnt, zero, offs, out
+):
+    nc = tc.nc
+    with ExitStack() as ctx:
+        keep = ctx.enter_context(tc.tile_pool(name="keep", bufs=1))
+        psum = ctx.enter_context(tc.psum_pool(name="psum", bufs=1))
+
+        def blk(i):
+            return slice(i * P, (i + 1) * P)
+
+        def work(name):
+            return [keep.tile([P, S], F32, name="%s%d" % (name, i)) for i in range(NB)]
+
+        def bank(group, i, name):
+            return psum.tile([P, S], F32, name=name, tag="bank_%s%d" % (group, i))
+
+        offsets = keep.tile([P, S // 16], U16, name="offsets")
+        x_win = keep.tile([P, T], I32, name="x_win")
+        e_win = keep.tile([P, T], I32, name="e_win")
+        xs_win = keep.tile([P, T], U8, name="xs_win")
+        es_win = keep.tile([P, T], U8, name="es_win")
+        th_win = keep.tile([P, T], F32, name="th_win")
+        h_raw = [keep.tile([P, PACK, HALF], F32, name="h_raw%d" % i, tag="slot_h_raw%d" % i) for i in range(2)]
+        h_bf = [keep.tile([P, HALF, PACK], BF16, name="h_bf%d" % i, align_bytes=64) for i in range(2)]
+        h_codes = keep.tile([P, V], U32, name="h_codes", align_bytes=64)
+        h_sc = keep.tile([P, V], U8, name="h_sc", align_bytes=64)
+        x_codes = keep.tile([P, S], U32, name="x_codes", align_bytes=64)
+        e_codes = keep.tile([P, S], U32, name="e_codes", align_bytes=64)
+        x_sc = keep.tile([P, S], U8, name="x_sc", align_bytes=64)
+        e_sc = keep.tile([P, S], U8, name="e_sc", align_bytes=64)
+        lib_sb = keep.tile([P, NB], F32, name="lib_sb")
+        cnt_sb = keep.tile([P, NB, S], F32, name="cnt_sb")
+        zero_sb = keep.tile([P, NB, S], F32, name="zero_sb")
+        ident = keep.tile([P, P], F32, name="ident")
+
+        def load_scales(win, scales):
+            for q in range(4):
+                nc.sync.dma_start(
+                    out=win[32 * q : 32 * q + 4, :].bitcast(I32),
+                    in_=scales[0, 4 * q : 4 * q + 4, :].bitcast(I32),
+                )
+
+        def load_words(win, words):
+            nc.sync.dma_start(out=win[:], in_=words[0].rearrange("p n t -> p (n t)").bitcast(I32))
+
+        h_rows = hT.rearrange("(p j) c -> p j c", j=PACK)
+
+        seed = keep.tile([P, 1], F32, name="seed")
+        nc.vector.memset(seed[:], 0.0)
+        nc.vector.memset(es_win[:].bitcast(I32), 0)
+        nc.vector.memset(xs_win[:].bitcast(I32), 0)
+        nc.gpsimd.memset(th_win[:], 0.0)
+        nc.sync.dma_start(offsets[:], offs)
+        nc.sync.dma_start(out=h_raw[0][:], in_=h_rows[:, :, 0:HALF])
+        load_scales(es_win, e_scales)
+        load_words(e_win, e_words)
+        nc.sync.dma_start(out=h_raw[1][:], in_=h_rows[:, :, HALF:V])
+        load_scales(xs_win, x_scales)
+        load_words(x_win, x_words)
+        nc.sync.dma_start(out=th_win[0:1, :], in_=theta[0:1, :])
+        with nc.allow_non_contiguous_dma(reason="one library size a partition"):
+            nc.sync.dma_start(out=lib_sb[:], in_=lib.rearrange("(t p) o -> p (t o)", p=P))
+        nc.sync.dma_start(out=cnt_sb[:], in_=cnt.rearrange("(t p) j -> p t j", p=P))
+        nc.sync.dma_start(out=zero_sb[:], in_=zero.rearrange("(t p) j -> p t j", p=P))
+        make_identity(nc, ident[:])
+
+        def interleave(i, copy):
+            copy(
+                out=h_bf[i][:].rearrange("p (c i) t -> p c t i", i=4),
+                in_=h_raw[i][:].rearrange("p t (c i) -> p c t i", i=4),
+            )
+
+        def quantize(i):
+            cols = slice(i * HALF, (i + 1) * HALF)
+            nc.vector.quantize_mx(
+                out=h_codes[:, cols].bitcast(FP8X4),
+                scales=h_sc[:, cols],
+                in_=h_bf[i][:].rearrange("p c t -> p (c t)"),
+            )
+
+        def gather(dst, win):
+            nc.vector.tensor_copy(dst[:], win.indirect(offsets[:]))
+
+        ex = work("ex")
+        warm = keep.tile([P, 3], F32, name="warm")
+        la, lb, ee = work("la"), work("lb"), work("ee")
+        u1, u2, nlc, ww = work("u1"), work("u2"), work("nlc"), work("ww")
+        t1, l0, t2, res = work("t1"), work("l0"), work("t2"), work("res")
+        nmax = keep.tile([P, NB, S], F32, name="nmax", tag="nmax_then_lc")
+        rsum = [keep.tile([P, 1], F32, name="rsum%d" % i) for i in range(NB)]
+        rinv = [keep.tile([P, 1], F32, name="rinv%d" % i) for i in range(NB)]
+
+        def dropout(i):
+            cols = slice(i * HALF, (i + 1) * HALF)
+            for pair in range(2):
+                pi = bank("lo", 2 * i + pair, "pi%d_%d" % (i, pair))
+                for n in range(2):
+                    g = 2 * pair + n
+                    nc.tensor.matmul_mx(
+                        out=pi[:, n * HALF : (n + 1) * HALF], lhsT=e_codes[:, blk(g)].bitcast(FP8X4), lhsT_scale=e_sc[:, blk(g)],
+                        rhs=h_codes[:, cols].bitcast(FP8X4), rhs_scale=h_sc[:, cols], start=True, stop=True,
+                    )
+                nc.scalar.activation(
+                    out=sg[:, 2 * pair : 2 * pair + 2, cols], in_=pi[:].rearrange("p (n c) -> p n c", n=2), func=ACT.Sigmoid
+                )
+
+        nc.scalar.activation(out=warm[:, 0:1], in_=seed[:], func=ACT.Sigmoid)
+        interleave(0, nc.scalar.copy)
+        gather(e_sc, es_win[:])
+        quantize(0)
+        gather(e_codes, e_win[:].bitcast(U32))
+        interleave(1, nc.scalar.copy)
+        sg = keep.tile([P, NB, V], F32, name="sg", tag="slot_h_raw1")
+        dropout(0)
+        quantize(1)
+        dropout(1)
+
+        gather(x_sc, xs_win[:])
+        gather(x_codes, x_win[:].bitcast(U32))
+        nc.scalar.activation(out=warm[:, 1:2], in_=sg[:, NB - 1, V - 1 : V], func=ACT.Exp)
+
+        for c in range(NB):
+            y = bank("hi", c, "y%d" % c)
+            nc.tensor.matmul_mx(
+                out=y[:], lhsT=h_codes[:, blk(c)].bitcast(FP8X4), lhsT_scale=h_sc[:, blk(c)],
+                rhs=x_codes[:].bitcast(FP8X4), rhs_scale=x_sc[:], start=True, stop=True,
+            )
+            nc.vector.tensor_reduce(out=nmax[:, c, 0:1], in_=y[:], axis=AX.X, op=ALU.max, negate=True)
+            nc.scalar.activation(out=ex[c][:], in_=y[:], func=ACT.Exp, bias=nmax[:, c, 0:1], scale=1.0, accum_out=rsum[c][:])
+
+        th_g = keep.tile([P, S], F32, name="th_g")
+        gather(th_g, th_win[:])
+        th_t = bank("lo", 3, "th_t")
+        for g in range(NB):
+            nc.tensor.transpose(th_t[:, blk(g)], th_g[:, blk(g)], ident[:])
+        th = keep.tile([P, NB], F32, name="th")
+        rth = keep.tile([P, NB], F32, name="rth")
+        nth = keep.tile([P, NB], F32, name="nth")
+        eth = keep.tile([P, NB], F32, name="eth")
+        nc.vector.tensor_copy(out=th[:], in_=th_t[:].rearrange("p (g m) -> p g m", m=P)[:, :, 0])
+        nc.vector.reciprocal(out=rth[:], in_=th[:])
+        nc.vector.tensor_scalar(out=nth[:], in0=th[:], scalar1=-1.0, scalar2=None, op0=ALU.mult)
+        nc.vector.tensor_scalar(out=eth[:], in0=rth[:], scalar1=0.001, scalar2=None, op0=ALU.mult)
+
+        mu = keep.tile([P, NB, S], F32, name="mu", tag="mu_then_q")
+        mu_t = [bank("lo", g, "mu_t%d" % g) for g in range(NB)]
+        for c in range(NB):
+            nc.vector.reciprocal(out=rinv[c][:], in_=rsum[c][:])
+            nc.vector.tensor_scalar(
+                out=mu[:, c, :], in0=ex[c][:], scalar1=rinv[c][:], scalar2=lib_sb[:, c : c + 1], op0=ALU.mult, op1=ALU.mult
+            )
+            for g in range(NB):
+                nc.tensor.transpose(mu_t[g][:, blk(c)], mu[:, c, blk(g)], ident[:])
+
+        cnt_t = []
+        for g in range(NB):
+            cnt_t.append(bank("hi", g, "cnt_t%d" % g))
+            for c in range(NB):
+                nc.tensor.transpose(cnt_t[g][:, blk(c)], cnt_sb[:, c, blk(g)], ident[:])
+
+        def by_cells(t):
+            return t.rearrange("p (c m) -> p c m", m=P)
+
+        def add_turned(acc, terms):
+            for c in range(NB):
+                for n, term in enumerate(terms):
+                    nc.tensor.matmul(
+                        acc[:, blk(c)], lhsT=term[:, blk(c)], rhs=ident[:],
+                        start=(n == 0), stop=(n == len(terms) - 1), is_transpose=True,
+                    )
+
+        lc = keep.tile([P, NB, S], F32, name="lc", tag="nmax_then_lc")
+        for g in range(NB):
+            col = slice(g, g + 1)
+            nc.scalar.activation(out=lc[:, g, :], in_=sg[:, g, :], func=ACT.Ln, bias=1.0001, scale=-1.0)
+            nc.scalar.activation(out=la[g][:], in_=mu_t[g][:], func=ACT.Ln, bias=1.0, scale=rth[:, col])
+            nc.scalar.activation(out=lb[g][:], in_=mu_t[g][:], func=ACT.Ln, bias=eth[:, col], scale=rth[:, col])
+            nc.gpsimd.tensor_scalar(out=nlc[g][:], in0=lc[:, g, :], scalar1=-1.0, scalar2=0.0, op0=ALU.mult, op1=ALU.add)
+            nc.vector.scalar_tensor_tensor(
+                out=u1[g][:], in0=cnt_t[g][:], scalar=th[:, col], in1=la[g][:], op0=ALU.add, op1=ALU.mult
+            )
+            nc.vector.scalar_tensor_tensor(
+                out=u2[g][:], in0=cnt_t[g][:], scalar=-1.0, in1=lb[g][:], op0=ALU.mult, op1=ALU.mult
+            )
+            nl1 = bank("lo", g, "nl1_%d" % g)
+            add_turned(nl1, [nlc[g], u1[g], u2[g]])
+            nc.vector.scalar_tensor_tensor(
+                out=by_cells(t1[g][:]), in0=zero_sb[:, :, blk(g)], scalar=1.0, in1=by_cells(nl1[:]),
+                op0=ALU.subtract, op1=ALU.mult,
+            )
+
+        q1 = keep.tile([P, NB, S], F32, name="q1", tag="mu_then_q")
+        for g in range(NB):
+            nc.gpsimd.tensor_scalar(out=q1[:, g, :], in0=sg[:, g, :], scalar1=-1.0, scalar2=1.0, op0=ALU.mult, op1=ALU.add)
+        for g in range(NB):
+            nc.scalar.activation(out=ee[g][:], in_=la[g][:], func=ACT.Exp, scale=nth[:, g : g + 1])
+        nc.scalar.activation(out=warm[:, 2:3], in_=ee[NB - 1][:, 0:1], func=ACT.Ln, bias=1.0)
+        mix = []
+        for g in range(NB):
+            nc.vector.tensor_tensor(out=ww[g][:], in0=ee[g][:], in1=q1[:, g, :], op=ALU.mult)
+            mix.append(bank("hi", g, "mix%d" % g))
+            add_turned(mix[g], [sg[:, g, :], ww[g]])
+
+        out_v = out.rearrange("(c p) j -> p c j", p=P)
+
+        def finish(g):
+            nc.vector.tensor_tensor(out=res[g][:], in0=t2[g][:], in1=t1[g][:], op=ALU.add)
+            nc.sync.dma_start(out=out_v[:, :, blk(g)], in_=by_cells(res[g][:]))
+
+        for g in range(NB):
+            nc.scalar.activation(out=l0[g][:], in_=mix[g][:], func=ACT.Ln)
+            nc.vector.tensor_tensor(out=by_cells(t2[g][:]), in0=by_cells(l0[g][:]), in1=zero_sb[:, :, blk(g)], op=ALU.mult)
+            if g > 0:
+                finish(g - 1)
+        finish(NB - 1)

@@ -65,8 +65,8 @@ def tile_picked_yzinb_ll_p_kernel(
         def load_scales(win, scales):
             for q in range(4):
                 nc.sync.dma_start(
-                    out=win[32 * q : 32 * q + 4, :].bitcast(I32),
-                    in_=scales[0, 4 * q : 4 * q + 4, :].bitcast(I32),
+                    out=win[q:P:32, :].bitcast(I32),
+                    in_=scales[0, q:16:4, :].bitcast(I32),
                 )
 
         def load_words(win, words):
@@ -75,10 +75,11 @@ def tile_picked_yzinb_ll_p_kernel(
         h_rows = hT.rearrange("(p j) c -> p j c", j=PACK)
 
         seed = keep.tile([P, 1], F32, name="seed")
-        nc.vector.memset(seed[:], 0.0)
         nc.vector.memset(es_win[:].bitcast(I32), 0)
+        nc.vector.memset(seed[:], 0.0)
         nc.vector.memset(xs_win[:].bitcast(I32), 0)
-        nc.gpsimd.memset(th_win[:], 0.0)
+        nc.vector.memset(th_win[:], 0.0)
+        nc.vector.memset(ident[:], 0.0)
         nc.sync.dma_start(offsets[:], offs)
         nc.sync.dma_start(out=h_raw[0][:], in_=h_rows[:, :, 0:HALF])
         load_scales(es_win, e_scales)
@@ -91,7 +92,7 @@ def tile_picked_yzinb_ll_p_kernel(
             nc.sync.dma_start(out=lib_sb[:], in_=lib.rearrange("(t p) o -> p (t o)", p=P))
         nc.sync.dma_start(out=cnt_sb[:], in_=cnt.rearrange("(t p) j -> p t j", p=P))
         nc.sync.dma_start(out=zero_sb[:], in_=zero.rearrange("(t p) j -> p t j", p=P))
-        make_identity(nc, ident[:])
+        make_identity(nc, ident[:], nomemset=True)
 
         def interleave(i, copy):
             copy(
@@ -202,17 +203,17 @@ def tile_picked_yzinb_ll_p_kernel(
         for g in range(NB):
             col = slice(g, g + 1)
             nc.scalar.activation(out=lc[:, g, :], in_=sg[:, g, :], func=ACT.Ln, bias=1.0001, scale=-1.0)
-            nc.scalar.activation(out=la[g][:], in_=mu_t[g][:], func=ACT.Ln, bias=1.0, scale=rth[:, col])
             nc.scalar.activation(out=lb[g][:], in_=mu_t[g][:], func=ACT.Ln, bias=eth[:, col], scale=rth[:, col])
-            nc.gpsimd.tensor_scalar(out=nlc[g][:], in0=lc[:, g, :], scalar1=-1.0, scalar2=0.0, op0=ALU.mult, op1=ALU.add)
-            nc.vector.scalar_tensor_tensor(
-                out=u1[g][:], in0=cnt_t[g][:], scalar=th[:, col], in1=la[g][:], op0=ALU.add, op1=ALU.mult
-            )
+            nc.scalar.activation(out=la[g][:], in_=mu_t[g][:], func=ACT.Ln, bias=1.0, scale=rth[:, col])
             nc.vector.scalar_tensor_tensor(
                 out=u2[g][:], in0=cnt_t[g][:], scalar=-1.0, in1=lb[g][:], op0=ALU.mult, op1=ALU.mult
             )
+            nc.gpsimd.tensor_tensor(out=nlc[g][:], in0=u2[g][:], in1=lc[:, g, :], op=ALU.subtract)
+            nc.vector.scalar_tensor_tensor(
+                out=u1[g][:], in0=cnt_t[g][:], scalar=th[:, col], in1=la[g][:], op0=ALU.add, op1=ALU.mult
+            )
             nl1 = bank("lo", g, "nl1_%d" % g)
-            add_turned(nl1, [nlc[g], u1[g], u2[g]])
+            add_turned(nl1, [u1[g], nlc[g]])
             nc.vector.scalar_tensor_tensor(
                 out=by_cells(t1[g][:]), in0=zero_sb[:, :, blk(g)], scalar=1.0, in1=by_cells(nl1[:]),
                 op0=ALU.subtract, op1=ALU.mult,

@@ -48,7 +48,7 @@ def tile_picked_yzinb_ll_p_kernel(
         e_win = keep.tile([P, T], I32, name="e_win")
         xs_win = keep.tile([P, T], U8, name="xs_win")
         es_win = keep.tile([P, T], U8, name="es_win")
-        th_win = keep.tile([P, T], F32, name="th_win")
+        th_win = keep.tile([P, T], F32, name="th_win", tag="slot_th_win")
         h_raw = [keep.tile([P, PACK, HALF], F32, name="h_raw%d" % i, tag="slot_h_raw%d" % i) for i in range(2)]
         h_bf = [keep.tile([P, HALF, PACK], BF16, name="h_bf%d" % i, align_bytes=64) for i in range(2)]
         h_codes = keep.tile([P, V], U32, name="h_codes", align_bytes=64)
@@ -168,11 +168,14 @@ def tile_picked_yzinb_ll_p_kernel(
         nth = keep.tile([P, NB], F32, name="nth")
         eth = keep.tile([P, NB], F32, name="eth")
         nc.vector.tensor_copy(out=th[:], in_=th_t[:].rearrange("p (g m) -> p g m", m=P)[:, :, 0])
+        q1 = keep.tile([P, NB, S], F32, name="q1", tag="slot_th_win")
+        for g in range(NB):
+            nc.gpsimd.tensor_scalar(out=q1[:, g, :], in0=sg[:, g, :], scalar1=-1.0, scalar2=1.0, op0=ALU.mult, op1=ALU.add)
         nc.vector.reciprocal(out=rth[:], in_=th[:])
         nc.vector.tensor_scalar(out=nth[:], in0=th[:], scalar1=-1.0, scalar2=None, op0=ALU.mult)
         nc.vector.tensor_scalar(out=eth[:], in0=rth[:], scalar1=0.001, scalar2=None, op0=ALU.mult)
 
-        mu = keep.tile([P, NB, S], F32, name="mu", tag="mu_then_q")
+        mu = keep.tile([P, NB, S], F32, name="mu")
         mu_t = [bank("lo", g, "mu_t%d" % g) for g in range(NB)]
         for c in range(NB):
             nc.vector.reciprocal(out=rinv[c][:], in_=rsum[c][:])
@@ -191,13 +194,14 @@ def tile_picked_yzinb_ll_p_kernel(
         def by_cells(t):
             return t.rearrange("p (c m) -> p c m", m=P)
 
-        def add_turned(acc, terms):
+        def turn(acc, term, first):
             for c in range(NB):
-                for n, term in enumerate(terms):
-                    nc.tensor.matmul(
-                        acc[:, blk(c)], lhsT=term[:, blk(c)], rhs=ident[:],
-                        start=(n == 0), stop=(n == len(terms) - 1), is_transpose=True,
-                    )
+                nc.tensor.matmul(
+                    acc[:, blk(c)], lhsT=term[:, blk(c)], rhs=ident[:],
+                    start=(first and c == 0), stop=(not first and c == NB - 1), is_transpose=True,
+                )
+
+        mix = []
 
         lc = keep.tile([P, NB, S], F32, name="lc", tag="nmax_then_lc")
         for g in range(NB):
@@ -213,33 +217,34 @@ def tile_picked_yzinb_ll_p_kernel(
                 out=u1[g][:], in0=cnt_t[g][:], scalar=th[:, col], in1=la[g][:], op0=ALU.add, op1=ALU.mult
             )
             nl1 = bank("lo", g, "nl1_%d" % g)
-            add_turned(nl1, [u1[g], nlc[g]])
+            turn(nl1, u1[g], True)
+            mix.append(bank("hi", g, "mix%d" % g))
+            turn(mix[g], sg[:, g, :], True)
+            turn(nl1, nlc[g], False)
             nc.vector.scalar_tensor_tensor(
                 out=by_cells(t1[g][:]), in0=zero_sb[:, :, blk(g)], scalar=1.0, in1=by_cells(nl1[:]),
                 op0=ALU.subtract, op1=ALU.mult,
             )
 
-        q1 = keep.tile([P, NB, S], F32, name="q1", tag="mu_then_q")
-        for g in range(NB):
-            nc.gpsimd.tensor_scalar(out=q1[:, g, :], in0=sg[:, g, :], scalar1=-1.0, scalar2=1.0, op0=ALU.mult, op1=ALU.add)
         for g in range(NB):
             nc.scalar.activation(out=ee[g][:], in_=la[g][:], func=ACT.Exp, scale=nth[:, g : g + 1])
         nc.scalar.activation(out=warm[:, 2:3], in_=ee[NB - 1][:, 0:1], func=ACT.Ln, bias=1.0)
-        mix = []
         for g in range(NB):
             nc.vector.tensor_tensor(out=ww[g][:], in0=ee[g][:], in1=q1[:, g, :], op=ALU.mult)
-            mix.append(bank("hi", g, "mix%d" % g))
-            add_turned(mix[g], [sg[:, g, :], ww[g]])
+            turn(mix[g], ww[g], False)
 
         out_v = out.rearrange("(c p) j -> p c j", p=P)
 
-        def finish(g):
-            nc.vector.tensor_tensor(out=res[g][:], in0=t2[g][:], in1=t1[g][:], op=ALU.add)
-            nc.sync.dma_start(out=out_v[:, :, blk(g)], in_=by_cells(res[g][:]))
+        def finish(g, parts):
+            n = NB // parts
+            for i in range(parts):
+                cols = slice(i * n * P, (i + 1) * n * P)
+                nc.vector.tensor_tensor(out=res[g][:, cols], in0=t2[g][:, cols], in1=t1[g][:, cols], op=ALU.add)
+                nc.sync.dma_start(out=out_v[:, i * n : (i + 1) * n, blk(g)], in_=by_cells(res[g][:, cols]))
 
         for g in range(NB):
             nc.scalar.activation(out=l0[g][:], in_=mix[g][:], func=ACT.Ln)
             nc.vector.tensor_tensor(out=by_cells(t2[g][:]), in0=by_cells(l0[g][:]), in1=zero_sb[:, :, blk(g)], op=ALU.mult)
             if g > 0:
-                finish(g - 1)
-        finish(NB - 1)
+                finish(g - 1, 1)
+        finish(NB - 1, 2)

from contextlib import ExitStack

import concourse.mybir as mybir
from concourse.masks import make_identity

F32 = mybir.dt.float32
BF16 = mybir.dt.bfloat16
I32 = mybir.dt.int32
U32 = mybir.dt.uint32
U16 = mybir.dt.uint16
U8 = mybir.dt.uint8
FP8X4 = mybir.dt.float8_e4m3fn_x4
ACT = mybir.ActivationFunctionType
ALU = mybir.AluOpType
AX = mybir.AxisListType

P = 128
K = 512
T = 2048
S = 512
V = 512
PACK = 4
NB = 4
HALF = V // 2

FLOPS = 2 * 2 * K * V * S


def tile_picked_yzinb_ll_p_kernel(
    tc, x_words, x_scales, hT, e_words, e_scales, lib, theta, cnt, zero, offs, out
):
    nc = tc.nc
    with ExitStack() as ctx:
        keep = ctx.enter_context(tc.tile_pool(name="keep", bufs=1))
        psum = ctx.enter_context(tc.psum_pool(name="psum", bufs=1))

        def blk(i):
            return slice(i * P, (i + 1) * P)

        def work(name):
            return [keep.tile([P, S], F32, name="%s%d" % (name, i)) for i in range(NB)]

        def bank(group, i, name):
            return psum.tile([P, S], F32, name=name, tag="bank_%s%d" % (group, i))

        offsets = keep.tile([P, S // 16], U16, name="offsets")
        x_win = keep.tile([P, T], I32, name="x_win")
        e_win = keep.tile([P, T], I32, name="e_win")
        xs_win = keep.tile([P, T], U8, name="xs_win")
        es_win = keep.tile([P, T], U8, name="es_win")
        th_win = keep.tile([P, T], F32, name="th_win", tag="slot_th_win")
        h_raw = [keep.tile([P, PACK, HALF], F32, name="h_raw%d" % i, tag="slot_h_raw%d" % i) for i in range(2)]
        h_bf = [keep.tile([P, HALF, PACK], BF16, name="h_bf%d" % i, align_bytes=64) for i in range(2)]
        h_codes = keep.tile([P, V], U32, name="h_codes", align_bytes=64)
        h_sc = keep.tile([P, V], U8, name="h_sc", align_bytes=64)
        x_codes = keep.tile([P, S], U32, name="x_codes", align_bytes=64)
        e_codes = keep.tile([P, S], U32, name="e_codes", align_bytes=64)
        x_sc = keep.tile([P, S], U8, name="x_sc", align_bytes=64)
        e_sc = keep.tile([P, S], U8, name="e_sc", align_bytes=64)
        lib_sb = keep.tile([P, NB], F32, name="lib_sb")
        cnt_sb = keep.tile([P, NB, S], F32, name="cnt_sb")
        zero_sb = keep.tile([P, NB, S], F32, name="zero_sb")
        ident = keep.tile([P, P], F32, name="ident")

        def load_scales(win, scales):
            for q in range(4):
                nc.sync.dma_start(
                    out=win[q:P:32, :].bitcast(I32),
                    in_=scales[0, q:16:4, :].bitcast(I32),
                )

        def load_words(win, words):
            nc.sync.dma_start(out=win[:], in_=words[0].rearrange("p n t -> p (n t)").bitcast(I32))

        h_rows = hT.rearrange("(p j) c -> p j c", j=PACK)

        seed = keep.tile([P, 1], F32, name="seed")
        nc.vector.memset(es_win[:].bitcast(I32), 0)
        nc.vector.memset(seed[:], 0.0)
        nc.vector.memset(xs_win[:].bitcast(I32), 0)
        nc.vector.memset(th_win[:], 0.0)
        nc.vector.memset(ident[:], 0.0)
        nc.sync.dma_start(offsets[:], offs)
        nc.sync.dma_start(out=h_raw[0][:], in_=h_rows[:, :, 0:HALF])
        load_scales(es_win, e_scales)
        load_words(e_win, e_words)
        nc.sync.dma_start(out=h_raw[1][:], in_=h_rows[:, :, HALF:V])
        load_scales(xs_win, x_scales)
        load_words(x_win, x_words)
        nc.sync.dma_start(out=th_win[0:1, :], in_=theta[0:1, :])
        with nc.allow_non_contiguous_dma(reason="one library size a partition"):
            nc.sync.dma_start(out=lib_sb[:], in_=lib.rearrange("(t p) o -> p (t o)", p=P))
        nc.sync.dma_start(out=cnt_sb[:], in_=cnt.rearrange("(t p) j -> p t j", p=P))
        nc.sync.dma_start(out=zero_sb[:], in_=zero.rearrange("(t p) j -> p t j", p=P))
        make_identity(nc, ident[:], nomemset=True)

        def interleave(i, copy):
            copy(
                out=h_bf[i][:].rearrange("p (c i) t -> p c t i", i=4),
                in_=h_raw[i][:].rearrange("p t (c i) -> p c t i", i=4),
            )

        def quantize(i):
            cols = slice(i * HALF, (i + 1) * HALF)
            nc.vector.quantize_mx(
                out=h_codes[:, cols].bitcast(FP8X4),
                scales=h_sc[:, cols],
                in_=h_bf[i][:].rearrange("p c t -> p (c t)"),
            )

        def gather(dst, win):
            nc.vector.tensor_copy(dst[:], win.indirect(offsets[:]))

        ex = work("ex")
        warm = keep.tile([P, 3], F32, name="warm")
        la, lb, ee = work("la"), work("lb"), work("ee")
        u1, u2, nlc, ww = work("u1"), work("u2"), work("nlc"), work("ww")
        t1, l0, t2, res = work("t1"), work("l0"), work("t2"), work("res")
        nmax = keep.tile([P, NB, S], F32, name="nmax", tag="nmax_then_lc")
        rsum = [keep.tile([P, 1], F32, name="rsum%d" % i) for i in range(NB)]
        rinv = [keep.tile([P, 1], F32, name="rinv%d" % i) for i in range(NB)]

        def dropout(i):
            cols = slice(i * HALF, (i + 1) * HALF)
            for pair in range(2):
                pi = bank("lo", 2 * i + pair, "pi%d_%d" % (i, pair))
                for n in range(2):
                    g = 2 * pair + n
                    nc.tensor.matmul_mx(
                        out=pi[:, n * HALF : (n + 1) * HALF], lhsT=e_codes[:, blk(g)].bitcast(FP8X4), lhsT_scale=e_sc[:, blk(g)],
                        rhs=h_codes[:, cols].bitcast(FP8X4), rhs_scale=h_sc[:, cols], start=True, stop=True,
                    )
                nc.scalar.activation(
                    out=sg[:, 2 * pair : 2 * pair + 2, cols], in_=pi[:].rearrange("p (n c) -> p n c", n=2), func=ACT.Sigmoid
                )

        nc.scalar.activation(out=warm[:, 0:1], in_=seed[:], func=ACT.Sigmoid)
        interleave(0, nc.scalar.copy)
        gather(e_sc, es_win[:])
        quantize(0)
        gather(e_codes, e_win[:].bitcast(U32))
        interleave(1, nc.scalar.copy)
        sg = keep.tile([P, NB, V], F32, name="sg", tag="slot_h_raw1")
        dropout(0)
        quantize(1)
        dropout(1)

        gather(x_sc, xs_win[:])
        gather(x_codes, x_win[:].bitcast(U32))
        nc.scalar.activation(out=warm[:, 1:2], in_=sg[:, NB - 1, V - 1 : V], func=ACT.Exp)

        for c in range(NB):
            y = bank("hi", c, "y%d" % c)
            nc.tensor.matmul_mx(
                out=y[:], lhsT=h_codes[:, blk(c)].bitcast(FP8X4), lhsT_scale=h_sc[:, blk(c)],
                rhs=x_codes[:].bitcast(FP8X4), rhs_scale=x_sc[:], start=True, stop=True,
            )
            nc.vector.tensor_reduce(out=nmax[:, c, 0:1], in_=y[:], axis=AX.X, op=ALU.max, negate=True)
            nc.scalar.activation(out=ex[c][:], in_=y[:], func=ACT.Exp, bias=nmax[:, c, 0:1], scale=1.0, accum_out=rsum[c][:])

        th_g = keep.tile([P, S], F32, name="th_g")
        gather(th_g, th_win[:])
        th_t = bank("lo", 3, "th_t")
        for g in range(NB):
            nc.tensor.transpose(th_t[:, blk(g)], th_g[:, blk(g)], ident[:])
        th = keep.tile([P, NB], F32, name="th")
        rth = keep.tile([P, NB], F32, name="rth")
        nth = keep.tile([P, NB], F32, name="nth")
        eth = keep.tile([P, NB], F32, name="eth")
        nc.vector.tensor_copy(out=th[:], in_=th_t[:].rearrange("p (g m) -> p g m", m=P)[:, :, 0])
        q1 = keep.tile([P, NB, S], F32, name="q1", tag="slot_th_win")
        for g in range(NB):
            nc.gpsimd.tensor_scalar(out=q1[:, g, :], in0=sg[:, g, :], scalar1=-1.0, scalar2=1.0, op0=ALU.mult, op1=ALU.add)
        nc.vector.reciprocal(out=rth[:], in_=th[:])
        nc.vector.tensor_scalar(out=nth[:], in0=th[:], scalar1=-1.0, scalar2=None, op0=ALU.mult)
        nc.vector.tensor_scalar(out=eth[:], in0=rth[:], scalar1=0.001, scalar2=None, op0=ALU.mult)

        mu = keep.tile([P, NB, S], F32, name="mu")
        mu_t = [bank("lo", g, "mu_t%d" % g) for g in range(NB)]
        for c in range(NB):
            nc.vector.reciprocal(out=rinv[c][:], in_=rsum[c][:])
            nc.vector.tensor_scalar(
                out=mu[:, c, :], in0=ex[c][:], scalar1=rinv[c][:], scalar2=lib_sb[:, c : c + 1], op0=ALU.mult, op1=ALU.mult
            )
            for g in range(NB):
                nc.tensor.transpose(mu_t[g][:, blk(c)], mu[:, c, blk(g)], ident[:])

        cnt_t = []
        for g in range(NB):
            cnt_t.append(bank("hi", g, "cnt_t%d" % g))
            for c in range(NB):
                nc.tensor.transpose(cnt_t[g][:, blk(c)], cnt_sb[:, c, blk(g)], ident[:])

        def by_cells(t):
            return t.rearrange("p (c m) -> p c m", m=P)

        def turn(acc, term, first):
            for c in range(NB):
                nc.tensor.matmul(
                    acc[:, blk(c)], lhsT=term[:, blk(c)], rhs=ident[:],
                    start=(first and c == 0), stop=(not first and c == NB - 1), is_transpose=True,
                )

        mix = []

        lc = keep.tile([P, NB, S], F32, name="lc", tag="nmax_then_lc")
        for g in range(NB):
            col = slice(g, g + 1)
            nc.scalar.activation(out=lc[:, g, :], in_=sg[:, g, :], func=ACT.Ln, bias=1.0001, scale=-1.0)
            nc.scalar.activation(out=lb[g][:], in_=mu_t[g][:], func=ACT.Ln, bias=eth[:, col], scale=rth[:, col])
            nc.scalar.activation(out=la[g][:], in_=mu_t[g][:], func=ACT.Ln, bias=1.0, scale=rth[:, col])
            nc.vector.scalar_tensor_tensor(
                out=u2[g][:], in0=cnt_t[g][:], scalar=-1.0, in1=lb[g][:], op0=ALU.mult, op1=ALU.mult
            )
            nc.gpsimd.tensor_tensor(out=nlc[g][:], in0=u2[g][:], in1=lc[:, g, :], op=ALU.subtract)
            nc.vector.scalar_tensor_tensor(
                out=u1[g][:], in0=cnt_t[g][:], scalar=th[:, col], in1=la[g][:], op0=ALU.add, op1=ALU.mult
            )
            nl1 = bank("lo", g, "nl1_%d" % g)
            turn(nl1, u1[g], True)
            mix.append(bank("hi", g, "mix%d" % g))
            turn(mix[g], sg[:, g, :], True)
            turn(nl1, nlc[g], False)
            nc.vector.scalar_tensor_tensor(
                out=by_cells(t1[g][:]), in0=zero_sb[:, :, blk(g)], scalar=1.0, in1=by_cells(nl1[:]),
                op0=ALU.subtract, op1=ALU.mult,
            )

        for g in range(NB):
            nc.scalar.activation(out=ee[g][:], in_=la[g][:], func=ACT.Exp, scale=nth[:, g : g + 1])
        nc.scalar.activation(out=warm[:, 2:3], in_=ee[NB - 1][:, 0:1], func=ACT.Ln, bias=1.0)
        for g in range(NB):
            nc.vector.tensor_tensor(out=ww[g][:], in0=ee[g][:], in1=q1[:, g, :], op=ALU.mult)
            turn(mix[g], ww[g], False)

        out_v = out.rearrange("(c p) j -> p c j", p=P)

        def finish(g, parts):
            n = NB // parts
            for i in range(parts):
                cols = slice(i * n * P, (i + 1) * n * P)
                nc.vector.tensor_tensor(out=res[g][:, cols], in0=t2[g][:, cols], in1=t1[g][:, cols], op=ALU.add)
                nc.sync.dma_start(out=out_v[:, i * n : (i + 1) * n, blk(g)], in_=by_cells(res[g][:, cols]))

        for g in range(NB):
            nc.scalar.activation(out=l0[g][:], in_=mix[g][:], func=ACT.Ln)
            nc.vector.tensor_tensor(out=by_cells(t2[g][:]), in0=by_cells(l0[g][:]), in1=zero_sb[:, :, blk(g)], op=ALU.mult)
            if g > 0:
                finish(g - 1, 1)
        finish(NB - 1, 2)
